import numpy as np
import ml_dtypes


def mxq(x, axis, fmt="e4m3"):
    dtype, down = {"e4m3": (ml_dtypes.float8_e4m3fn, 7), "e5m2": (ml_dtypes.float8_e5m2, 14)}[fmt]
    v = np.moveaxis(np.asarray(x, np.float32).astype(ml_dtypes.bfloat16).astype(np.float64), axis, -1)
    blocks = v.reshape(v.shape[:-1] + (-1, 32))
    amax = np.abs(blocks).max(-1, keepdims=True)
    byte = np.maximum(np.where(amax > 0, np.frexp(amax)[1] - 1 + 127, 0) - down, 1)
    scale = np.exp2(byte - 127.0)
    codes = (blocks / scale).astype(np.float32).astype(dtype).astype(np.float64)
    return np.moveaxis((codes * scale).reshape(v.shape), -1, axis)


WIDE = False


def mx_kscale(k):
    if not WIDE:
        return np.ones(k)
    levels = np.array([10, -10, 5, -5, 0])
    if k % 512:
        return np.exp2(np.random.permutation(np.resize(levels, k // 32))).repeat(32)
    a = np.empty((k // 512, 16))
    for p in range(k // 512):
        a[p, :8] = np.random.permutation(np.resize(levels, 8))
        for g in range(8):
            far = levels[np.abs(levels - a[p, g]) >= 10]
            a[p, g + 8] = far[np.random.randint(len(far))]
    return np.exp2(a.ravel()).repeat(32)


def f64(x):
    return np.asarray(x).astype(np.float64)


def striped8(idx):
    return np.asarray(idx).reshape(8, -1, 16).transpose(0, 2, 1).reshape(128, -1).astype(np.uint16)


def unstriped8(offs):
    return offs.reshape(8, 16, -1).transpose(0, 2, 1).reshape(8, -1).astype(np.int64)


def pick8(x, idx, run):
    r = np.arange(len(x))
    return x[r[:, None], idx[r % (8 * run) // run]]


E2M1 = np.array([0.0, 0.5, 1.0, 1.5, 2.0, 3.0, 4.0, 6.0, -0.0, -0.5, -1.0, -1.5, -2.0, -3.0, -4.0, -6.0])


def pack_weight(w, fmt):
    k, n = w.shape
    w = f64(np.asarray(w, np.float32).astype(ml_dtypes.bfloat16)).reshape(k // 32, 32, n)
    amax = np.abs(w).max(1)
    if fmt == "e4m3":
        byte = np.frexp(amax)[1] - 1 + 127 - 7
    else:
        mant, ex = np.frexp(amax / 6.0)
        byte = np.where(mant > 0.5, ex, ex - 1) + 127
    byte = np.clip(np.where(amax > 0, byte, 1), 1, 254)
    scaled = (w * np.exp2(127.0 - byte)[:, None, :]).reshape(k, n).astype(np.float32)
    by_word = np.ascontiguousarray(scaled.reshape(k // 512, 128, 4, n).transpose(0, 1, 3, 2))
    if fmt == "e4m3":
        words = by_word.astype(ml_dtypes.float8_e4m3fn).view(np.uint8)
    else:
        c = by_word.astype(ml_dtypes.float4_e2m1fn).view(np.uint8) & 0xF
        words = (c[..., 0::2] | (c[..., 1::2] << 4)).reshape(k // 512, 128, 2 * n)
    return np.ascontiguousarray(words), np.ascontiguousarray(byte.astype(np.uint8).reshape(k // 512, 16, n))


def unpack_weight(words, scales, fmt):
    g, _, n = scales.shape
    words = np.ascontiguousarray(words).reshape(g, 128, n, -1)
    if fmt == "e4m3":
        vals = words.view(ml_dtypes.float8_e4m3fn).astype(np.float64)
    else:
        nib = np.empty((g, 128, n, 4), np.uint8)
        nib[..., 0::2] = words & 0xF
        nib[..., 1::2] = words >> 4
        vals = E2M1[nib]
    vals = vals * np.repeat(np.exp2(scales.astype(np.float64) - 127.0), 8, axis=1)[..., None]
    return vals.transpose(0, 1, 3, 2).reshape(g * 512, n)


D, T, I, Q = 512, 1024, 512, 128


def setup_inputs():
    n = np.random.standard_normal
    idx = np.stack([np.random.permutation(T)[:I] for _ in range(8)])
    idx2 = np.stack([np.random.permutation(T)[:I] for _ in range(8)])
    idx3 = np.stack([np.random.permutation(T)[:I] for _ in range(8)])
    idx4 = np.stack([np.random.permutation(T)[:I] for _ in range(8)])
    idx5 = np.stack([np.random.permutation(T)[:I] for _ in range(8)])
    idx6 = np.stack([np.random.permutation(T)[:I] for _ in range(8)])
    fd = mx_kscale(D)
    keysp = pack_weight(n((D, T)) / fd[:, None], "e2m1")
    return {
        "query": (n((D, Q)) * 1.0 / np.sqrt(D) * fd[:, None]).astype(np.float32),
        "keys_words": keysp[0],
        "keys_scales": keysp[1],
        "offs": striped8(idx),
        "offs2": striped8(idx2),
        "offs3": striped8(idx3),
        "offs4": striped8(idx4),
        "offs5": striped8(idx5),
        "offs6": striped8(idx6),
    }


def reference(query, keys_words, keys_scales, offs, offs2, offs3, offs4, offs5, offs6):
    idx = unstriped8(offs)
    idx2 = unstriped8(offs2)
    idx3 = unstriped8(offs3)
    idx4 = unstriped8(offs4)
    idx5 = unstriped8(offs5)
    idx6 = unstriped8(offs6)
    keysu = unpack_weight(keys_words, keys_scales, "e2m1")
    queryq = mxq(f64(query), 0, "e4m3")
    a = queryq.T @ keysu
    f1 = np.zeros((Q, T))
    f1[np.arange(Q)[:, None], idx2[np.arange(Q) % 128 // 16]] = pick8(a, idx, 16)
    c1 = a + f1
    w = np.minimum(pick8(c1, idx3, 16), pick8(c1, idx4, 16))
    f2 = np.zeros((Q, T))
    f2[np.arange(Q)[:, None], idx5[np.arange(Q) % 128 // 16]] = w
    c2 = c1 + f2
    y = pick8(c2, idx6, 16)
    return y

@@ -1,0 +1,111 @@
+from contextlib import ExitStack
+
+import concourse.mybir as mybir
+
+F32 = mybir.dt.float32
+BF16 = mybir.dt.bfloat16
+I32 = mybir.dt.int32
+U32 = mybir.dt.uint32
+U16 = mybir.dt.uint16
+U8 = mybir.dt.uint8
+FP8X4 = mybir.dt.float8_e4m3fn_x4
+FP4X4 = mybir.dt.float4_e2m1fn_x4
+ADD = mybir.AluOpType.add
+MIN = mybir.AluOpType.min
+COPY = mybir.ActivationFunctionType.Copy
+
+P = 128
+D, T, SLOTS, Q = 512, 1024, 512, 128
+PACK = 4
+N_PASS = 256
+HALF = SLOTS // 2
+HALF_COLS = HALF // 16
+FLOPS = 2 * D * T * Q
+
+
+def tile_attend_chained_one_kernel(tc, query, keys_words, keys_scales, offs, offs2, offs3, offs4, offs5, offs6, out):
+    nc = tc.nc
+    with ExitStack() as ctx:
+        keep = ctx.enter_context(tc.tile_pool(name="keep", bufs=1))
+        psum = ctx.enter_context(tc.psum_pool(name="psum", bufs=1))
+
+        q_raw = keep.tile([P, PACK, Q], F32, name="q_raw")
+        nc.sync.dma_start(out=q_raw[:], in_=query.rearrange("(p j) c -> p j c", j=PACK))
+        k_scales = keep.tile([P, T], U8, name="k_scales", align_bytes=64)
+        nc.vector.memset(k_scales[:].bitcast(I32), 0)
+        for quad in range(4):
+            nc.sync.dma_start(
+                out=k_scales[32 * quad : 32 * quad + 4, :].bitcast(I32),
+                in_=keys_scales[0, 4 * quad : 4 * quad + 4, :].bitcast(I32),
+            )
+
+        k_words = keep.tile([P, 2 * T], U8, name="k_words", align_bytes=64)
+        nc.sync.dma_start(out=k_words[:].bitcast(I32), in_=keys_words[0].bitcast(I32))
+
+        lists = []
+        for n, src in enumerate((offs, offs2, offs3, offs4, offs5, offs6)):
+            lst = keep.tile([P, SLOTS // 16], U16, name="list%d" % (n + 1))
+            nc.sync.dma_start(lst[:], src)
+            lists.append(lst)
+        l1, l2, l3, l4, l5, l6 = lists
+        first = slice(0, HALF_COLS)
+        second = slice(HALF_COLS, 2 * HALF_COLS)
+
+        f1 = keep.tile([P, T], F32, name="f1")
+        f2 = keep.tile([P, T], F32, name="f2")
+        nc.vector.memset(f1[:], 0.0)
+        nc.gpsimd.memset(f2[:], 0.0)
+
+        q_bf = keep.tile([P, Q, PACK], BF16, name="q_bf", align_bytes=64)
+        nc.vector.tensor_copy(out=q_bf[:], in_=q_raw[:].rearrange("p j c -> p c j"))
+        q_codes = keep.tile([P, Q], U32, name="q_codes", align_bytes=64)
+        q_scales = keep.tile([P, Q], U8, name="q_scales", align_bytes=64)
+        nc.vector.quantize_mx(out=q_codes[:].bitcast(FP8X4), scales=q_scales[:], in_=q_bf[:].rearrange("p c j -> p (c j)"))
+
+        a = keep.tile([P, T], F32, name="a")
+        for b in range(T // N_PASS):
+            bank = psum.tile([P, N_PASS], F32, name="bank%d" % b)
+            cols = slice(b * N_PASS, (b + 1) * N_PASS)
+            nc.tensor.matmul_mx(
+                out=bank[:],
+                lhsT=q_codes[:].bitcast(FP8X4),
+                lhsT_scale=q_scales[:],
+                rhs=k_words[:, 2 * b * N_PASS : 2 * (b + 1) * N_PASS].bitcast(FP4X4),
+                rhs_scale=k_scales[:, cols],
+                start=True,
+                stop=True,
+            )
+            if b % 2 == 0:
+                nc.scalar.copy(out=a[:, cols], in_=bank[:])
+            else:
+                nc.vector.tensor_copy(out=a[:, cols], in_=bank[:])
+
+        picked = keep.tile([P, SLOTS], F32, name="picked")
+        nc.vector.tensor_copy(picked[:, :HALF], a[:].indirect(l1[:, first]))
+        nc.scalar.activation(picked[:, HALF:], a[:].indirect(l1[:, second]), COPY)
+        nc.vector.tensor_copy(f1[:].indirect(l2[:]), picked[:])
+
+        c1 = keep.tile([P, T], F32, name="c1")
+        nc.vector.tensor_tensor(c1[:], a[:], f1[:], ADD)
+
+        g3 = keep.tile([P, SLOTS], F32, name="g3")
+        g4 = keep.tile([P, SLOTS], F32, name="g4")
+        w = keep.tile([P, SLOTS], F32, name="w")
+        nc.vector.tensor_copy(g3[:, :HALF], c1[:].indirect(l3[:, first]))
+        nc.scalar.activation(g4[:, :HALF], c1[:].indirect(l4[:, first]), COPY)
+        nc.scalar.activation(g3[:, HALF:], c1[:].indirect(l3[:, second]), COPY)
+        nc.scalar.activation(g4[:, HALF:], c1[:].indirect(l4[:, second]), COPY)
+        nc.vector.tensor_tensor(w[:, :HALF], g3[:, :HALF], g4[:, :HALF], MIN)
+        nc.vector.tensor_copy(f2[:].indirect(l5[:, first]), w[:, :HALF])
+        nc.vector.tensor_tensor(w[:, HALF:], g3[:, HALF:], g4[:, HALF:], MIN)
+        nc.vector.tensor_copy(f2[:].indirect(l5[:, second]), w[:, HALF:])
+
+        c2 = keep.tile([P, T], F32, name="c2")
+        nc.vector.tensor_tensor(c2[:], c1[:], f2[:], ADD)
+
+        y0 = keep.tile([P, HALF], F32, name="y0")
+        y1 = keep.tile([P, HALF], F32, name="y1")
+        nc.vector.tensor_copy(y0[:], c2[:].indirect(l6[:, first]))
+        nc.scalar.activation(y1[:], c2[:].indirect(l6[:, second]), COPY)
+        nc.sync.dma_start(out=out[:, :HALF], in_=y0[:])
+        nc.scalar.dma_start(out=out[:, HALF:], in_=y1[:])

@@ -1,6 +1,7 @@
 from contextlib import ExitStack
 
 import concourse.mybir as mybir
+from concourse.masks import make_identity
 
 F32 = mybir.dt.float32
 BF16 = mybir.dt.bfloat16
@@ -17,9 +18,11 @@ COPY = mybir.ActivationFunctionType.Copy
 P = 128
 D, T, SLOTS, Q = 512, 1024, 512, 128
 PACK = 4
-N_PASS = 256
 HALF = SLOTS // 2
 HALF_COLS = HALF // 16
+V_COLS_1 = 704
+V_BLOCKS_2 = 6
+PASSES = ((0, 512), (512, 768), (768, 896), (896, 1024))
 FLOPS = 2 * D * T * Q
 
 
@@ -31,16 +34,16 @@ def tile_attend_chained_one_kernel(tc, query, keys_words, keys_scales, offs, off
 
         q_raw = keep.tile([P, PACK, Q], F32, name="q_raw")
         nc.sync.dma_start(out=q_raw[:], in_=query.rearrange("(p j) c -> p j c", j=PACK))
+        k_words = keep.tile([P, 2 * T], U8, name="k_words", align_bytes=64)
+        nc.sync.dma_start(out=k_words[:].bitcast(I32), in_=keys_words[0].bitcast(I32))
+
         k_scales = keep.tile([P, T], U8, name="k_scales", align_bytes=64)
         nc.vector.memset(k_scales[:].bitcast(I32), 0)
         for quad in range(4):
-            nc.sync.dma_start(
+            nc.scalar.dma_start(
                 out=k_scales[32 * quad : 32 * quad + 4, :].bitcast(I32),
                 in_=keys_scales[0, 4 * quad : 4 * quad + 4, :].bitcast(I32),
             )
-
-        k_words = keep.tile([P, 2 * T], U8, name="k_words", align_bytes=64)
-        nc.sync.dma_start(out=k_words[:].bitcast(I32), in_=keys_words[0].bitcast(I32))
 
         lists = []
         for n, src in enumerate((offs, offs2, offs3, offs4, offs5, offs6)):
@@ -54,28 +57,36 @@ def tile_attend_chained_one_kernel(tc, query, keys_words, keys_scales, offs, off
         f1 = keep.tile([P, T], F32, name="f1")
         f2 = keep.tile([P, T], F32, name="f2")
         nc.vector.memset(f1[:], 0.0)
-        nc.gpsimd.memset(f2[:], 0.0)
+        nc.vector.memset(f2[:], 0.0)
 
         q_bf = keep.tile([P, Q, PACK], BF16, name="q_bf", align_bytes=64)
-        nc.vector.tensor_copy(out=q_bf[:], in_=q_raw[:].rearrange("p j c -> p c j"))
+        q_halves = (slice(0, Q // 2), slice(Q // 2, Q))
+        for h in q_halves:
+            nc.vector.tensor_copy(out=q_bf[:, h, :], in_=q_raw[:, :, h].rearrange("p j c -> p c j"))
         q_codes = keep.tile([P, Q], U32, name="q_codes", align_bytes=64)
         q_scales = keep.tile([P, Q], U8, name="q_scales", align_bytes=64)
-        nc.vector.quantize_mx(out=q_codes[:].bitcast(FP8X4), scales=q_scales[:], in_=q_bf[:].rearrange("p c j -> p (c j)"))
+        for h in q_halves:
+            nc.vector.quantize_mx(out=q_codes[:, h].bitcast(FP8X4), scales=q_scales[:, h], in_=q_bf[:, h, :].rearrange("p c j -> p (c j)"))
+
+        ident = keep.tile([P, P], F32, name="ident")
+        make_identity(nc, ident[:])
 
         a = keep.tile([P, T], F32, name="a")
-        for b in range(T // N_PASS):
-            bank = psum.tile([P, N_PASS], F32, name="bank%d" % b)
-            cols = slice(b * N_PASS, (b + 1) * N_PASS)
+        banks = []
+        for b, (lo, hi) in enumerate(PASSES):
+            bank = psum.tile([P, hi - lo], F32, name="bank%d" % b)
+            banks.append(bank)
+            cols = slice(lo, hi)
             nc.tensor.matmul_mx(
                 out=bank[:],
                 lhsT=q_codes[:].bitcast(FP8X4),
                 lhsT_scale=q_scales[:],
-                rhs=k_words[:, 2 * b * N_PASS : 2 * (b + 1) * N_PASS].bitcast(FP4X4),
+                rhs=k_words[:, 2 * lo : 2 * hi].bitcast(FP4X4),
                 rhs_scale=k_scales[:, cols],
                 start=True,
                 stop=True,
             )
-            if b % 2 == 0:
+            if b in (0, 3):
                 nc.scalar.copy(out=a[:, cols], in_=bank[:])
             else:
                 nc.vector.tensor_copy(out=a[:, cols], in_=bank[:])
@@ -86,7 +97,11 @@ def tile_attend_chained_one_kernel(tc, query, keys_words, keys_scales, offs, off
         nc.vector.tensor_copy(f1[:].indirect(l2[:]), picked[:])
 
         c1 = keep.tile([P, T], F32, name="c1")
-        nc.vector.tensor_tensor(c1[:], a[:], f1[:], ADD)
+        for b, (lo, hi) in enumerate(PASSES):
+            hi = min(hi, V_COLS_1)
+            if hi > lo:
+                nc.vector.tensor_tensor(c1[:, lo:hi], banks[b][:, : hi - lo], f1[:, lo:hi], ADD)
+        nc.gpsimd.tensor_tensor(c1[:, V_COLS_1:], a[:, V_COLS_1:], f1[:, V_COLS_1:], ADD)
 
         g3 = keep.tile([P, SLOTS], F32, name="g3")
         g4 = keep.tile([P, SLOTS], F32, name="g4")
@@ -100,8 +115,20 @@ def tile_attend_chained_one_kernel(tc, query, keys_words, keys_scales, offs, off
         nc.vector.tensor_tensor(w[:, HALF:], g3[:, HALF:], g4[:, HALF:], MIN)
         nc.vector.tensor_copy(f2[:].indirect(l5[:, second]), w[:, HALF:])
 
+        c1_t = keep.tile([P, V_BLOCKS_2 * P], F32, name="c1_t")
+        spans = [(lo, min(lo + 4, V_BLOCKS_2)) for lo in range(0, V_BLOCKS_2, 4)]
+        for lo, hi in spans:
+            turned = psum.tile([P, (hi - lo) * P], F32, name="turned%d" % lo)
+            for k in range(lo, hi):
+                nc.tensor.transpose(turned[:, (k - lo) * P : (k - lo + 1) * P], c1[:, k * P : (k + 1) * P], ident[:])
+            nc.scalar.copy(out=c1_t[:, lo * P : hi * P], in_=turned[:])
         c2 = keep.tile([P, T], F32, name="c2")
-        nc.vector.tensor_tensor(c2[:], c1[:], f2[:], ADD)
+        for lo, hi in spans:
+            back = psum.tile([P, (hi - lo) * P], F32, name="back%d" % lo)
+            for k in range(lo, hi):
+                nc.tensor.transpose(back[:, (k - lo) * P : (k - lo + 1) * P], c1_t[:, k * P : (k + 1) * P], ident[:])
+            nc.vector.tensor_tensor(c2[:, lo * P : hi * P], back[:], f2[:, lo * P : hi * P], ADD)
+        nc.gpsimd.tensor_tensor(c2[:, V_BLOCKS_2 * P :], c1[:, V_BLOCKS_2 * P :], f2[:, V_BLOCKS_2 * P :], ADD)
 
         y0 = keep.tile([P, HALF], F32, name="y0")
         y1 = keep.tile([P, HALF], F32, name="y1")

@@ -35,15 +35,17 @@ def tile_attend_chained_one_kernel(tc, query, keys_words, keys_scales, offs, off
         q_raw = keep.tile([P, PACK, Q], F32, name="q_raw")
         nc.sync.dma_start(out=q_raw[:], in_=query.rearrange("(p j) c -> p j c", j=PACK))
         k_words = keep.tile([P, 2 * T], U8, name="k_words", align_bytes=64)
-        nc.sync.dma_start(out=k_words[:].bitcast(I32), in_=keys_words[0].bitcast(I32))
+        nc.sync.dma_start(out=k_words[:, :T].bitcast(I32), in_=keys_words[0, :, :T].bitcast(I32))
 
         k_scales = keep.tile([P, T], U8, name="k_scales", align_bytes=64)
         nc.vector.memset(k_scales[:].bitcast(I32), 0)
         for quad in range(4):
-            nc.scalar.dma_start(
+            nc.sync.dma_start(
                 out=k_scales[32 * quad : 32 * quad + 4, :].bitcast(I32),
                 in_=keys_scales[0, 4 * quad : 4 * quad + 4, :].bitcast(I32),
             )
+
+        nc.sync.dma_start(out=k_words[:, T:].bitcast(I32), in_=keys_words[0, :, T:].bitcast(I32))
 
         lists = []
         for n, src in enumerate((offs, offs2, offs3, offs4, offs5, offs6)):

@@ -56,22 +56,26 @@ def tile_attend_chained_one_kernel(tc, query, keys_words, keys_scales, offs, off
         first = slice(0, HALF_COLS)
         second = slice(HALF_COLS, 2 * HALF_COLS)
 
+        ident = keep.tile([P, P], F32, name="ident")
+        nc.vector.memset(ident[:], 0.0)
+        make_identity(nc, ident[:], nomemset=True)
         f1 = keep.tile([P, T], F32, name="f1")
-        f2 = keep.tile([P, T], F32, name="f2")
         nc.vector.memset(f1[:], 0.0)
-        nc.vector.memset(f2[:], 0.0)
 
-        q_bf = keep.tile([P, Q, PACK], BF16, name="q_bf", align_bytes=64)
+        q_bf = keep.tile([P, Q, PACK], BF16, name="q_bf", tag="q_bf_then_f2", align_bytes=64)
         q_halves = (slice(0, Q // 2), slice(Q // 2, Q))
         for h in q_halves:
-            nc.vector.tensor_copy(out=q_bf[:, h, :], in_=q_raw[:, :, h].rearrange("p j c -> p c j"))
+            nc.vector.tensor_copy(
+                out=q_bf[:, h, :].rearrange("p (g i) j -> p g j i", i=PACK),
+                in_=q_raw[:, :, h].rearrange("p j (g i) -> p g j i", i=PACK),
+            )
         q_codes = keep.tile([P, Q], U32, name="q_codes", align_bytes=64)
         q_scales = keep.tile([P, Q], U8, name="q_scales", align_bytes=64)
         for h in q_halves:
             nc.vector.quantize_mx(out=q_codes[:, h].bitcast(FP8X4), scales=q_scales[:, h], in_=q_bf[:, h, :].rearrange("p c j -> p (c j)"))
 
-        ident = keep.tile([P, P], F32, name="ident")
-        make_identity(nc, ident[:])
+        f2 = keep.tile([P, T], F32, name="f2", tag="q_bf_then_f2", align_bytes=64)
+        nc.vector.memset(f2[:], 0.0)
 
         a = keep.tile([P, T], F32, name="a")
         banks = []
@@ -129,8 +133,9 @@ def tile_attend_chained_one_kernel(tc, query, keys_words, keys_scales, offs, off
             back = psum.tile([P, (hi - lo) * P], F32, name="back%d" % lo)
             for k in range(lo, hi):
                 nc.tensor.transpose(back[:, (k - lo) * P : (k - lo + 1) * P], c1_t[:, k * P : (k + 1) * P], ident[:])
-            nc.vector.tensor_tensor(c2[:, lo * P : hi * P], back[:], f2[:, lo * P : hi * P], ADD)
-        nc.gpsimd.tensor_tensor(c2[:, V_BLOCKS_2 * P :], c1[:, V_BLOCKS_2 * P :], f2[:, V_BLOCKS_2 * P :], ADD)
+            end = min(hi * P, V_COLS_1)
+            nc.vector.tensor_tensor(c2[:, lo * P : end], back[:, : end - lo * P], f2[:, lo * P : end], ADD)
+        nc.gpsimd.tensor_tensor(c2[:, V_COLS_1:], c1[:, V_COLS_1:], f2[:, V_COLS_1:], ADD)
 
         y0 = keep.tile([P, HALF], F32, name="y0")
         y1 = keep.tile([P, HALF], F32, name="y1")

@@ -116,10 +116,11 @@ def tile_attend_chained_one_kernel(tc, query, keys_words, keys_scales, offs, off
         nc.scalar.activation(g4[:, :HALF], c1[:].indirect(l4[:, first]), COPY)
         nc.scalar.activation(g3[:, HALF:], c1[:].indirect(l3[:, second]), COPY)
         nc.scalar.activation(g4[:, HALF:], c1[:].indirect(l4[:, second]), COPY)
-        nc.vector.tensor_tensor(w[:, :HALF], g3[:, :HALF], g4[:, :HALF], MIN)
-        nc.vector.tensor_copy(f2[:].indirect(l5[:, first]), w[:, :HALF])
+        nc.vector.tensor_tensor(w[:, :128], g3[:, :128], g4[:, :128], MIN)
+        nc.vector.tensor_tensor(w[:, 128:HALF], g3[:, 128:HALF], g4[:, 128:HALF], MIN)
+        nc.vector.tensor_copy(f2[:].indirect(l5[:, 0:8]), w[:, :128])
         nc.vector.tensor_tensor(w[:, HALF:], g3[:, HALF:], g4[:, HALF:], MIN)
-        nc.vector.tensor_copy(f2[:].indirect(l5[:, second]), w[:, HALF:])
+        nc.vector.tensor_copy(f2[:].indirect(l5[:, 8:32]), w[:, 128:])
 
         c1_t = keep.tile([P, V_BLOCKS_2 * P], F32, name="c1_t")
         spans = [(lo, min(lo + 4, V_BLOCKS_2)) for lo in range(0, V_BLOCKS_2, 4)]

from contextlib import ExitStack

import concourse.mybir as mybir
from concourse.masks import make_identity

F32 = mybir.dt.float32
BF16 = mybir.dt.bfloat16
I32 = mybir.dt.int32
U32 = mybir.dt.uint32
U16 = mybir.dt.uint16
U8 = mybir.dt.uint8
FP8X4 = mybir.dt.float8_e4m3fn_x4
FP4X4 = mybir.dt.float4_e2m1fn_x4
ADD = mybir.AluOpType.add
MIN = mybir.AluOpType.min
COPY = mybir.ActivationFunctionType.Copy

P = 128
D, T, SLOTS, Q = 512, 1024, 512, 128
PACK = 4
HALF = SLOTS // 2
HALF_COLS = HALF // 16
V_COLS_1 = 704
V_BLOCKS_2 = 6
PASSES = ((0, 512), (512, 768), (768, 896), (896, 1024))
FLOPS = 2 * D * T * Q


def tile_attend_chained_one_kernel(tc, query, keys_words, keys_scales, offs, offs2, offs3, offs4, offs5, offs6, out):
    nc = tc.nc
    with ExitStack() as ctx:
        keep = ctx.enter_context(tc.tile_pool(name="keep", bufs=1))
        psum = ctx.enter_context(tc.psum_pool(name="psum", bufs=1))

        q_raw = keep.tile([P, PACK, Q], F32, name="q_raw")
        nc.sync.dma_start(out=q_raw[:], in_=query.rearrange("(p j) c -> p j c", j=PACK))
        k_words = keep.tile([P, 2 * T], U8, name="k_words", align_bytes=64)
        nc.sync.dma_start(out=k_words[:, :T].bitcast(I32), in_=keys_words[0, :, :T].bitcast(I32))

        k_scales = keep.tile([P, T], U8, name="k_scales", align_bytes=64)
        nc.vector.memset(k_scales[:].bitcast(I32), 0)
        for quad in range(4):
            nc.sync.dma_start(
                out=k_scales[32 * quad : 32 * quad + 4, :].bitcast(I32),
                in_=keys_scales[0, 4 * quad : 4 * quad + 4, :].bitcast(I32),
            )

        nc.sync.dma_start(out=k_words[:, T:].bitcast(I32), in_=keys_words[0, :, T:].bitcast(I32))

        lists = []
        for n, src in enumerate((offs, offs2, offs3, offs4, offs5, offs6)):
            lst = keep.tile([P, SLOTS // 16], U16, name="list%d" % (n + 1))
            nc.sync.dma_start(lst[:], src)
            lists.append(lst)
        l1, l2, l3, l4, l5, l6 = lists
        first = slice(0, HALF_COLS)
        second = slice(HALF_COLS, 2 * HALF_COLS)

        ident = keep.tile([P, P], F32, name="ident")
        nc.vector.memset(ident[:], 0.0)
        make_identity(nc, ident[:], nomemset=True)
        f1 = keep.tile([P, T], F32, name="f1")
        nc.vector.memset(f1[:], 0.0)

        q_bf = keep.tile([P, Q, PACK], BF16, name="q_bf", tag="q_bf_then_f2", align_bytes=64)
        q_halves = (slice(0, Q // 2), slice(Q // 2, Q))
        for h in q_halves:
            nc.vector.tensor_copy(
                out=q_bf[:, h, :].rearrange("p (g i) j -> p g j i", i=PACK),
                in_=q_raw[:, :, h].rearrange("p j (g i) -> p g j i", i=PACK),
            )
        q_codes = keep.tile([P, Q], U32, name="q_codes", align_bytes=64)
        q_scales = keep.tile([P, Q], U8, name="q_scales", align_bytes=64)
        for h in q_halves:
            nc.vector.quantize_mx(out=q_codes[:, h].bitcast(FP8X4), scales=q_scales[:, h], in_=q_bf[:, h, :].rearrange("p c j -> p (c j)"))

        f2 = keep.tile([P, T], F32, name="f2", tag="q_bf_then_f2", align_bytes=64)
        nc.vector.memset(f2[:], 0.0)

        a = keep.tile([P, T], F32, name="a")
        banks = []
        for b, (lo, hi) in enumerate(PASSES):
            bank = psum.tile([P, hi - lo], F32, name="bank%d" % b)
            banks.append(bank)
            cols = slice(lo, hi)
            nc.tensor.matmul_mx(
                out=bank[:],
                lhsT=q_codes[:].bitcast(FP8X4),
                lhsT_scale=q_scales[:],
                rhs=k_words[:, 2 * lo : 2 * hi].bitcast(FP4X4),
                rhs_scale=k_scales[:, cols],
                start=True,
                stop=True,
            )
            if b in (0, 3):
                nc.scalar.copy(out=a[:, cols], in_=bank[:])
            else:
                nc.vector.tensor_copy(out=a[:, cols], in_=bank[:])

        picked = keep.tile([P, SLOTS], F32, name="picked")
        nc.vector.tensor_copy(picked[:, :HALF], a[:].indirect(l1[:, first]))
        nc.scalar.activation(picked[:, HALF:], a[:].indirect(l1[:, second]), COPY)
        nc.vector.tensor_copy(f1[:].indirect(l2[:]), picked[:])

        c1 = keep.tile([P, T], F32, name="c1")
        for b, (lo, hi) in enumerate(PASSES):
            hi = min(hi, V_COLS_1)
            if hi > lo:
                nc.vector.tensor_tensor(c1[:, lo:hi], banks[b][:, : hi - lo], f1[:, lo:hi], ADD)
        nc.gpsimd.tensor_tensor(c1[:, V_COLS_1:], a[:, V_COLS_1:], f1[:, V_COLS_1:], ADD)

        g3 = keep.tile([P, SLOTS], F32, name="g3")
        g4 = keep.tile([P, SLOTS], F32, name="g4")
        w = keep.tile([P, SLOTS], F32, name="w")
        nc.vector.tensor_copy(g3[:, :HALF], c1[:].indirect(l3[:, first]))
        nc.scalar.activation(g4[:, :HALF], c1[:].indirect(l4[:, first]), COPY)
        nc.scalar.activation(g3[:, HALF:], c1[:].indirect(l3[:, second]), COPY)
        nc.scalar.activation(g4[:, HALF:], c1[:].indirect(l4[:, second]), COPY)
        nc.vector.tensor_tensor(w[:, :128], g3[:, :128], g4[:, :128], MIN)
        nc.vector.tensor_tensor(w[:, 128:HALF], g3[:, 128:HALF], g4[:, 128:HALF], MIN)
        nc.vector.tensor_copy(f2[:].indirect(l5[:, 0:8]), w[:, :128])
        nc.vector.tensor_tensor(w[:, HALF:], g3[:, HALF:], g4[:, HALF:], MIN)
        nc.vector.tensor_copy(f2[:].indirect(l5[:, 8:32]), w[:, 128:])

        c1_t = keep.tile([P, V_BLOCKS_2 * P], F32, name="c1_t")
        spans = [(lo, min(lo + 4, V_BLOCKS_2)) for lo in range(0, V_BLOCKS_2, 4)]
        for lo, hi in spans:
            turned = psum.tile([P, (hi - lo) * P], F32, name="turned%d" % lo)
            for k in range(lo, hi):
                nc.tensor.transpose(turned[:, (k - lo) * P : (k - lo + 1) * P], c1[:, k * P : (k + 1) * P], ident[:])
            nc.scalar.copy(out=c1_t[:, lo * P : hi * P], in_=turned[:])
        c2 = keep.tile([P, T], F32, name="c2")
        for lo, hi in spans:
            back = psum.tile([P, (hi - lo) * P], F32, name="back%d" % lo)
            for k in range(lo, hi):
                nc.tensor.transpose(back[:, (k - lo) * P : (k - lo + 1) * P], c1_t[:, k * P : (k + 1) * P], ident[:])
            end = min(hi * P, V_COLS_1)
            nc.vector.tensor_tensor(c2[:, lo * P : end], back[:, : end - lo * P], f2[:, lo * P : end], ADD)
        nc.gpsimd.tensor_tensor(c2[:, V_COLS_1:], c1[:, V_COLS_1:], f2[:, V_COLS_1:], ADD)

        y0 = keep.tile([P, HALF], F32, name="y0")
        y1 = keep.tile([P, HALF], F32, name="y1")
        nc.vector.tensor_copy(y0[:], c2[:].indirect(l6[:, first]))
        nc.scalar.activation(y1[:], c2[:].indirect(l6[:, second]), COPY)
        nc.sync.dma_start(out=out[:, :HALF], in_=y0[:])
        nc.scalar.dma_start(out=out[:, HALF:], in_=y1[:])
